import numpy as np
import ml_dtypes


def mxq(x, axis, fmt="e4m3"):
    dtype, down = {"e4m3": (ml_dtypes.float8_e4m3fn, 7), "e5m2": (ml_dtypes.float8_e5m2, 14)}[fmt]
    v = np.moveaxis(np.asarray(x, np.float32).astype(ml_dtypes.bfloat16).astype(np.float64), axis, -1)
    blocks = v.reshape(v.shape[:-1] + (-1, 32))
    amax = np.abs(blocks).max(-1, keepdims=True)
    byte = np.maximum(np.where(amax > 0, np.frexp(amax)[1] - 1 + 127, 0) - down, 1)
    scale = np.exp2(byte - 127.0)
    codes = (blocks / scale).astype(np.float32).astype(dtype).astype(np.float64)
    return np.moveaxis((codes * scale).reshape(v.shape), -1, axis)


WIDE = False


def mx_kscale(k):
    if not WIDE:
        return np.ones(k)
    levels = np.array([10, -10, 5, -5, 0])
    if k % 512:
        return np.exp2(np.random.permutation(np.resize(levels, k // 32))).repeat(32)
    a = np.empty((k // 512, 16))
    for p in range(k // 512):
        a[p, :8] = np.random.permutation(np.resize(levels, 8))
        for g in range(8):
            far = levels[np.abs(levels - a[p, g]) >= 10]
            a[p, g + 8] = far[np.random.randint(len(far))]
    return np.exp2(a.ravel()).repeat(32)


BF16 = ml_dtypes.bfloat16


def bf(x):
    return np.asarray(x, np.float32).astype(BF16)


def f64(x):
    return np.asarray(x).astype(np.float64)


E2M1 = np.array([0.0, 0.5, 1.0, 1.5, 2.0, 3.0, 4.0, 6.0, -0.0, -0.5, -1.0, -1.5, -2.0, -3.0, -4.0, -6.0])


def pack_weight(w, fmt):
    k, n = w.shape
    w = f64(bf(w)).reshape(k // 32, 32, n)
    amax = np.abs(w).max(1)
    if fmt == "e4m3":
        byte = np.frexp(amax)[1] - 1 + 127 - 7
    else:
        mant, ex = np.frexp(amax / 6.0)
        byte = np.where(mant > 0.5, ex, ex - 1) + 127
    byte = np.clip(np.where(amax > 0, byte, 1), 1, 254)
    scaled = (w * np.exp2(127.0 - byte)[:, None, :]).reshape(k, n).astype(np.float32)
    by_word = np.ascontiguousarray(scaled.reshape(k // 512, 128, 4, n).transpose(0, 1, 3, 2))
    if fmt == "e4m3":
        words = by_word.astype(ml_dtypes.float8_e4m3fn).view(np.uint8)
    else:
        c = by_word.astype(ml_dtypes.float4_e2m1fn).view(np.uint8) & 0xF
        words = c[..., 0::2] | (c[..., 1::2] << 4)
    return np.ascontiguousarray(words), np.ascontiguousarray(byte.astype(np.uint8).reshape(k // 512, 16, n))


def unpack_weight(words, scales, fmt):
    g, p, n, _ = words.shape
    if fmt == "e4m3":
        vals = np.ascontiguousarray(words).view(ml_dtypes.float8_e4m3fn).astype(np.float64)
    else:
        nib = np.empty((g, p, n, 4), np.uint8)
        nib[..., 0::2] = words & 0xF
        nib[..., 1::2] = words >> 4
        vals = E2M1[nib]
    vals = vals * np.repeat(np.exp2(scales.astype(np.float64) - 127.0), 8, axis=1)[..., None]
    return vals.transpose(0, 1, 3, 2).reshape(g * 512, n)
def pack4(w):
    words, scales = pack_weight(w, "e2m1")
    return words.reshape(words.shape[0], 128, -1), scales


def unpack4(words, scales):
    return unpack_weight(words.reshape(words.shape[0], 128, -1, 2), scales, "e2m1")


def planes(Y):
    n, m = Y.shape
    b = f64(bf(Y)).reshape(n // 32, 32, m)
    amax = np.abs(b).max(1)
    byte = np.clip(np.where(amax > 0, np.frexp(amax)[1] - 1 + 127 - 7, 1), 1, 254)
    codes = (b * np.exp2(127.0 - byte)[:, None, :]).reshape(n, m).astype(np.float32).astype(ml_dtypes.float8_e4m3fn).view(np.uint8)
    words = codes.reshape(n // 512, 128, 4, m).transpose(0, 1, 3, 2)
    return np.ascontiguousarray(words), np.ascontiguousarray(byte.astype(np.uint8).reshape(n // 512, 16, m))


E, K, L, P, Q = 2048, 1536, 1024, 512, 1024
CAUCHY = 2.3849

def setup_inputs():
    noise = np.random.randn
    s1, s2, t = mx_kscale(K), mx_kscale(L), mx_kscale(E)
    F1 = noise(K, E) * s1[:, None] * t[None, :]
    A2 = noise(E, L) * s2[None, :] / t[:, None]
    B1 = noise(K, P) * K ** -0.5 * E ** -0.25 / s1[:, None]
    B2 = noise(L, Q) * L ** -0.5 * E ** -0.25 / s2[:, None]
    f1_words, f1_scales = pack_weight(F1, "e4m3")
    b2_words, b2_scales = pack4(B2)
    return {"f1_words": f1_words, "f1_scales": f1_scales, "B1": bf(B1), "A2": bf(A2),
            "b2_words": b2_words, "b2_scales": b2_scales,
            "info": bf(np.exp(0.4 * noise(E))), "resid": bf(2.0 * noise(E)),
            "H0": bf(0.4 * noise(P, Q)),
            "unit1": bf(np.exp(0.3 * noise(P))), "unit2": bf(np.exp(0.8 * noise(Q)))}

def reference(f1_words, f1_scales, B1, A2, b2_words, b2_scales, info, resid, H0, unit1, unit2):
    J1 = unpack_weight(f1_words, f1_scales, "e4m3").T @ mxq(f64(B1), 0, "e4m3")
    J2 = mxq(f64(A2), 1, "e4m3") @ unpack4(b2_words, b2_scales)
    w = 1.0 / (1.0 + (f64(resid) / CAUCHY) ** 2)
    V1 = J1 * f64(info)[:, None]
    V2 = J2 * w[:, None]
    H = mxq(V1, 0, "e4m3").T @ mxq(V2, 0, "e4m3")
    y = (H + f64(H0)) * f64(unit1)[:, None] * f64(unit2)[None, :]
    words, scales = planes(y.T)
    return y, words, scales

@@ -1,0 +1,669 @@
+from contextlib import ExitStack
+
+import concourse.mybir as mybir
+from concourse.masks import make_identity
+
+E, K, L, P, Q = 2048, 1536, 1024, 512, 1024
+CAUCHY = 2.3849
+FLOPS = 2 * E * (K * P + L * Q + P * Q)
+
+F32 = mybir.dt.float32
+BF16 = mybir.dt.bfloat16
+I32 = mybir.dt.int32
+U32 = mybir.dt.uint32
+U8 = mybir.dt.uint8
+FP8X4 = mybir.dt.float8_e4m3fn_x4
+FP4X4 = mybir.dt.float4_e2m1fn_x4
+ALU = mybir.AluOpType
+ACT = mybir.ActivationFunctionType
+
+NP = 128
+EG, KG, LG, QG, PT = E // 512, K // 512, L // 512, Q // 512, P // NP
+UNIT1_ROW = 32
+
+
+SPLIT = 0
+
+
+def program_order():
+    o = []
+
+    def put(*steps):
+        o.extend(steps)
+
+    put(("load", "vec", 0), ("load", "vec", 1), ("ident",))
+    put(("warm_prep",), ("clear", "b2s", "V"), ("warm_quant",), ("warm", 10, 0))
+    put(("clear", "vec", "V"), ("clear", "f1s", "V"))
+    put(("load", "a2", 0, 0), ("load", "vec", 2), *[("load", "a2", 0, t) for t in (1, 2, 3)])
+    put(("load", "b2w", 0), *[("load", "b2s", i) for i in range(4)], ("load", "b2w", 1))
+    put(*[("load", "a2", 1, t) for t in range(4)])
+    put(("load", "b1", 0), ("load", "b1", 1))
+    put(*[("load", "a2", 2, t) for t in range(4)])
+    put(("load", "b1", 2), *[("load", "f1s", i) for i in range(4)])
+    put(("load", "f1", 0), *[("load", "a2", 3, t) for t in range(4)])
+    put(("load", "f1", 1), ("load", "f1", 2), ("load", "f1", 3), ("load", "h0"), ("load", "u2"))
+
+    def split(g):
+        if SPLIT and g >= SPLIT - 1:
+            for t in range(4):
+                put(("a2_split", g, t, "SSSS"[t]))
+
+    def turn(g):
+        for t in range(4):
+            put(("a2_turn", g, t), ("a2_out", g, t))
+
+    def j2_pair(g, c):
+        put(("j2", g, (c, c + 1)), ("j2_out", g, c), ("j2_out", g, c + 1))
+
+    def j1_slots(g, ts):
+        for t in ts:
+            put(("j1", g, t), ("j1_out", g, t))
+
+    def j1_half(g, half):
+        for tp in range(2):
+            put(("j1h", g, half, tp), ("j1h_out", g, half, tp))
+        put(("v1_weave", g, half, "S"))
+
+    put(("vec_stage",))
+    for t in range(4):
+        if t == 3:
+            put(("vec_turn",))
+        put(("a2_turn", 0, t), ("a2_out", 0, t), ("a2_quant", 0, (t,)))
+    put(("vec_out",))
+    for t in range(4):
+        put(("j2t", 0, (0, 1, 2, 3), t))
+    split(1)
+    put(*[("j2_out", 0, c) for c in range(4)])
+    put(("j2", 0, (4, 5)))
+    turn(1)
+    put(("j2_out", 0, 4), ("j2_out", 0, 5), ("a2_quant", 1, (0, 1)), ("a2_quant", 1, (2, 3)))
+    put(("b1_weave", 0, "S"))
+    split(2)
+    j2_pair(0, 6)
+    put(("b1_weave", 1, "S"))
+    j2_pair(1, 0)
+    put(("b1_weave", 2, "V"), ("b1_quant", 0))
+    j2_pair(1, 2)
+    turn(2)
+    put(("b1_quant", 2), ("f1_scales",), ("f1_words", 0), ("b1_quant", 1))
+    split(3)
+    j2_pair(1, 4)
+    put(("v2_quant", 0, (0, 1, 2, 3)))
+    put(("a2_quant", 2, (0, 1)), ("a2_quant", 2, (2, 3)))
+    j2_pair(1, 6)
+    put(("v2_quant", 0, (4, 5, 6, 7)), ("f1_words", 1))
+    j1_slots(0, range(4))
+    turn(3)
+    put(("v1_weave", 0, 0, "S"), ("v1_weave", 0, 1, "S"), ("v2_quant", 1, (0, 1, 2, 3)), ("f1_words", 2))
+    j2_pair(2, 0)
+    put(("v2_quant", 1, (4, 5, 6, 7)), ("a2_quant", 3, (0, 1)), ("a2_quant", 3, (2, 3)), ("v1_quant", 0, (0, 1)))
+    j1_slots(1, range(4))
+    put(("v1_weave", 1, 0, "S"), ("v1_weave", 1, 1, "S"), ("f1_words", 3))
+
+    def j1_pair(g, half, tp):
+        put(("j1h", g, half, tp), ("j1h_out", g, half, tp))
+        if tp == 1:
+            put(("v1_weave", g, half, "S"))
+
+    j2_pair(2, 2)
+    j1_pair(2, 0, 0)
+    j2_pair(2, 4)
+    put(("v2_quant", 2, (0, 1, 2, 3)))
+    j1_pair(2, 0, 1)
+    j2_pair(2, 6)
+    put(("v1_quant", 1, (0, 1)))
+    j1_pair(3, 0, 0)
+    j2_pair(3, 0)
+    put(("v2_quant", 2, (4, 5, 6, 7)))
+    j1_pair(3, 0, 1)
+    j2_pair(3, 2)
+    put(("v1_quant", 2, (0,)))
+    j2_pair(3, 4)
+    put(("v2_quant", 3, (0, 1, 2, 3)), ("v1_quant", 3, (0,)))
+    j1_pair(2, 1, 0)
+    j2_pair(3, 6)
+    j1_pair(2, 1, 1)
+
+    def passes(h, j):
+        put(("h", h, j, (0, 1, 2, 3)), ("h_add", h, j))
+
+    def finish(h, j, eng="y_scale"):
+        put((eng, h, j), ("y_round", h, j), ("y_store", h, j))
+
+    def planes(h, tiles):
+        put(("y_turn", h, tiles), ("y_out", h, tiles))
+
+    def planes_out(h, tiles):
+        put(("y_quant", h, tiles), ("words_store", h, tiles))
+
+    def epilogue(h, j, add="h_add"):
+        put((add, h, j, 0), (add, h, j, 1), ("y_scale", h, j, 0), ("y_scale", h, j, 1))
+
+    def whole(h, j):
+        put(("h", h, j, (0, 1, 2, 3)))
+        epilogue(h, j)
+        put(("y_round", h, j), ("y_store", h, j))
+
+    passes(0, 0)
+    put(("v2_quant", 3, (4, 5, 6, 7)))
+    j1_pair(3, 1, 0)
+    j1_pair(3, 1, 1)
+    put(("y_scale", 0, 0), ("v1_quant", 2, (1,)), ("y_round", 0, 0), ("y_store", 0, 0))
+    whole(0, 1)
+    put(("h", 1, 0, (0, 1, 2, 3)), ("h_add", 1, 0), ("v1_quant", 3, (1,)))
+    finish(1, 0)
+    whole(1, 1)
+    whole(0, 2)
+    put(("h", 0, 3, (0, 1, 2, 3)))
+    epilogue(0, 3)
+    put(("h", 1, 2, (0, 1, 2, 3)))
+    planes(0, (0, 1))
+    put(("y_turn", 1, (0, 1)), ("y_round", 0, 3), ("y_store", 0, 3), ("y_out", 1, (0, 1)))
+    epilogue(1, 2)
+    put(("hh", 1, 3, 0), ("hh", 1, 3, 1), ("y_turn", 0, (2, 3)))
+    put(("y_round", 1, 2), ("y_store", 1, 2), ("y_out", 0, (2, 3)), ("y_turn", 1, (2,)), ("y_out", 1, (2,)))
+    put(("hh_add", 1, 3, 0), ("hh_add", 1, 3, 1), ("y_quant", 0, (0, 1)), ("words_store", 0, (0, 1)), ("y_direct", 1, 3, 0), ("y_direct", 1, 3, 1))
+    planes(1, (3,))
+    put(("y_scale", 1, 3), ("y_store", 1, 3))
+    planes_out(1, (0, 1))
+    put(("y_quant", 0, (2, 3)), ("words_store", 0, (2, 3)))
+    put(("y_quant", 1, (2, 3)), ("words_store", 1, (2, 3)))
+    put(*[("scales_store", (0, 1), i) for i in range(4)])
+    return o
+
+
+def tile_robust_information_block_k4_kernel(
+    tc, f1_words, f1_scales, B1, A2, b2_words, b2_scales, info, resid, H0, unit1, unit2, out_0, out_1, out_2
+):
+    nc = tc.nc
+    with ExitStack() as ctx:
+        keep = ctx.enter_context(tc.tile_pool(name="keep", bufs=1))
+        psum = ctx.enter_context(tc.psum_pool(name="psum", bufs=1))
+        ctx.enter_context(tc.manual_schedule())
+
+        def sbuf(name, shape, dtype, tag=None):
+            return keep.tile(shape, dtype, name=name, tag=tag or name, align_bytes=64)
+
+        late = {}
+
+        def reuse(name, shape, dtype, tag):
+            if name not in late:
+                late[name] = sbuf(name, shape, dtype, tag)
+            return late[name]
+
+        banks = [psum.tile([NP, 512], F32, name="bank%d" % b) for b in range(8)]
+        bank_of = {}
+
+        def next_bank(key):
+            bank_of[key] = banks[len(bank_of) % len(banks)]
+            return bank_of[key]
+
+        ident = sbuf("ident", [NP, NP], F32)
+        vec_raw = sbuf("vec_raw", [NP, 512], BF16)
+        vec_rows = sbuf("vec_rows", [NP, 4, NP], F32)
+        vec_cols = sbuf("vec_cols", [NP, 4, UNIT1_ROW + 1], F32)
+        cauchy_sq = sbuf("cauchy_sq", [NP, EG, 4], F32)
+        cauchy_den = sbuf("cauchy_den", [NP, EG, 4], F32)
+        weight = sbuf("weight", [NP, EG, 4], F32)
+
+        a2_raw = [sbuf("a2_raw%d" % g, [NP, 4, L], BF16) for g in range(EG)]
+        a2_even_odd = sbuf("a2_even_odd", [NP, 2, 4, L // 2], F32) if SPLIT else None
+        a2_turned = sbuf("a2_turned", [NP, 2, 4 * LG * NP * 4], BF16)
+        a2_codes = sbuf("a2_codes", [NP, 2, 4 * LG * NP], U32)
+        a2_scales = sbuf("a2_scales", [NP, 2, 4 * LG * NP], U8)
+        b2_codes = sbuf("b2_codes", [NP, LG, 2 * Q], U8)
+        b2_plane = sbuf("b2_plane", [NP, LG, Q], U8)
+
+        f1_raw = [sbuf("f1_raw%d" % g, [NP, KG * 512], I32) for g in range(EG)]
+        f1_codes = sbuf("f1_codes", [NP, 2, 4, KG, NP], I32)
+        f1_plane_raw = sbuf("f1_plane_raw", [NP, E], U8)
+        f1_plane = sbuf("f1_plane", [NP, 4, EG, NP], U8)
+        b1_raw = sbuf("b1_raw", [NP, KG, 4, P], BF16)
+        b1_woven = sbuf("b1_woven", [NP, KG, P * 4], BF16)
+        b1_codes = sbuf("b1_codes", [NP, KG, P], U32)
+        b1_scales = sbuf("b1_scales", [NP, KG, P], U8)
+
+        v1_slots = sbuf("v1_slots", [NP, 2, 4, P], BF16)
+        v1_woven = sbuf("v1_woven", [NP, 2, P * 4], BF16)
+        v1_codes = sbuf("v1_codes", [NP, EG, P], U32)
+        v1_scales = sbuf("v1_scales", [NP, EG, P], U8)
+        v2_slots = sbuf("v2_slots", [NP, 4, 512], BF16) if any(s[0] == "j2w" for s in program_order()) else None
+        v2_woven = sbuf("v2_woven", [NP, 2, Q * 4], BF16)
+        v2_codes = sbuf("v2_codes", [NP, EG, Q], U32)
+        v2_scales = sbuf("v2_scales", [NP, EG, Q], U8)
+
+        h0 = sbuf("h0", [NP, PT, Q], BF16)
+        unit2_rows = sbuf("unit2_rows", [NP, Q], BF16)
+        h_sum = sbuf("h_sum", [NP, 2, 512], F32)
+
+        def y_of(h):
+            return reuse("y%d" % h, [NP, PT, 512], F32, "a2_raw%d" % h)
+
+        def y_round():
+            return reuse("y_round", [NP, QG, PT, 512], BF16, "a2_raw2")
+
+        def y_turned():
+            return reuse("y_turned", [NP, QG, P * 4], BF16, "a2_raw3")
+
+        y_codes = sbuf("y_codes", [NP, QG, P], U32)
+        y_scales = sbuf("y_scales", [NP, QG, P], U8)
+
+        def copy_on(engine, out, in_):
+            if engine == "S":
+                nc.scalar.copy(out=out, in_=in_)
+            else:
+                nc.vector.tensor_copy(out=out, in_=in_)
+
+        def weave(engine, woven, slots):
+            copy_on(
+                engine,
+                woven.rearrange("p (c i t) -> p c t i", i=4, t=4),
+                slots.rearrange("p t (c i) -> p c t i", i=4),
+            )
+
+        def quantize(codes, scales, values):
+            nc.vector.quantize_mx(out=codes.bitcast(FP8X4), scales=scales, in_=values)
+
+        def load(name, i=0, t=0):
+            if name == "vec":
+                src = [info, resid, unit1][i]
+                rows = [slice(0, EG), slice(EG, 2 * EG), slice(UNIT1_ROW, UNIT1_ROW + 1)][i]
+                queue = nc.gpsimd if i < 2 else nc.sync
+                queue.dma_start(out=vec_raw[rows, :], in_=src.rearrange("(g e) -> g e", e=512))
+            elif name == "a2":
+                rows = A2[512 * i : 512 * (i + 1), :].rearrange("(j t i) k -> t j i k", t=4, i=8)
+                nc.sync.dma_start(out=a2_raw[i][:, t, :], in_=rows[t])
+            elif name == "b2w":
+                cols = slice(256 * i, 256 * (i + 1))
+                nc.sync.dma_start(
+                    out=b2_codes[:].bitcast(I32)[:, :, cols],
+                    in_=b2_words.bitcast(I32).rearrange("g p n -> p g n")[:, :, cols],
+                )
+            elif name == "b2s":
+                nc.sync.dma_start(
+                    out=b2_plane[32 * i : 32 * i + 4].bitcast(I32),
+                    in_=b2_scales.bitcast(I32).rearrange("g r n -> r g n")[4 * i : 4 * i + 4],
+                )
+            elif name == "b1":
+                nc.sync.dma_start(
+                    out=b1_raw[:, i], in_=B1[512 * i : 512 * (i + 1), :].rearrange("(p t) c -> p t c", t=4)
+                )
+            elif name == "f1":
+                words = f1_words.rearrange("g p n t -> p g (n t)").bitcast(I32)
+                nc.sync.dma_start(
+                    out=f1_raw[i][:].rearrange("p (g n) -> p g n", g=KG),
+                    in_=words[:, :, 512 * i : 512 * (i + 1)],
+                )
+            elif name == "f1s":
+                nc.sync.dma_start(
+                    out=f1_plane_raw[32 * i : 32 * i + 4 * KG, :].bitcast(I32),
+                    in_=f1_scales.bitcast(I32)[:, 4 * i : 4 * i + 4, :],
+                )
+            elif name == "h0":
+                nc.sync.dma_start(out=h0[:], in_=H0.rearrange("(j p) q -> p j q", p=NP))
+            else:
+                nc.sync.dma_start(out=unit2_rows[:], in_=unit2.partition_broadcast(NP))
+
+        def clear(name, engine):
+            eng = nc.vector if engine == "V" else nc.gpsimd
+            if name == "b2s":
+                eng.memset(b2_plane[:].bitcast(I32), 0)
+            elif name == "f1s":
+                eng.memset(f1_plane_raw[:].bitcast(I32), 0)
+            else:
+                eng.memset(vec_rows[:], 0.0)
+
+        def ident_step():
+            make_identity(nc, ident[:])
+
+        def warm_prep():
+            nc.vector.memset(reuse("warm_zeros", [NP, 512], BF16, None)[:], 0.0)
+
+        def warm_quant():
+            quantize(
+                reuse("warm_codes", [NP, NP], U32, None)[:],
+                reuse("warm_scales", [NP, NP], U8, None)[:],
+                late["warm_zeros"][:],
+            )
+
+        def warm(count, n):
+            bank = next_bank(("warm", n))
+            codes = late["warm_codes"][:].bitcast(FP8X4)
+            scales = late["warm_scales"][:]
+            for i in range(count):
+                nc.tensor.matmul_mx(
+                    out=bank[:, 0:NP], lhsT=codes, lhsT_scale=scales, rhs=codes, rhs_scale=scales,
+                    start=(i == 0), stop=(i == count - 1),
+                )
+
+        def vec_stage():
+            nc.vector.tensor_copy(
+                out=vec_rows[0 : 2 * EG].rearrange("p t (j i) -> p t j i", i=8),
+                in_=vec_raw[0 : 2 * EG, :].rearrange("p (j t i) -> p t j i", t=4, i=8),
+            )
+            row = slice(UNIT1_ROW, UNIT1_ROW + 1)
+            nc.vector.tensor_copy(out=vec_rows[row].rearrange("p t c -> p (t c)"), in_=vec_raw[row, :])
+
+        def vec_turn():
+            bank = next_bank("vec")
+            for t in range(4):
+                nc.tensor.transpose(bank[:, NP * t : NP * (t + 1)], vec_rows[:, t, :], ident[:])
+
+        def vec_out():
+            bank = bank_of["vec"][:].rearrange("p (t c) -> p t c", t=4)
+            nc.vector.tensor_copy(out=vec_cols[:], in_=bank[:, :, 0 : UNIT1_ROW + 1])
+            r = vec_cols[:, :, EG : 2 * EG].rearrange("p t g -> p g t")
+            nc.vector.scalar_tensor_tensor(
+                out=cauchy_sq[:], in0=r, scalar=1.0 / (CAUCHY * CAUCHY), in1=r, op0=ALU.mult, op1=ALU.mult
+            )
+            nc.vector.tensor_scalar_add(out=cauchy_den[:], in0=cauchy_sq[:], scalar1=1.0)
+            nc.vector.reciprocal(out=weight[:], in_=cauchy_den[:])
+
+        def a2_split(g, t, engine):
+            copy_on(
+                engine,
+                a2_even_odd[:, g % 2, t, :].rearrange("p (l u m) -> p l u m", l=LG, u=2),
+                a2_raw[g][:, t, :].bitcast(F32).rearrange("p (l m u) -> p l u m", l=LG, u=2),
+            )
+
+        def a2_turn(g, t):
+            bank = next_bank(("a2", g, t))
+            words = a2_raw[g][:, t, :].bitcast(F32)
+            for l in range(LG):
+                for u in range(2):
+                    s = 2 * l + u
+                    if SPLIT and g >= SPLIT - 1:
+                        src = a2_even_odd[:, g % 2, t, NP * s : NP * (s + 1)]
+                    else:
+                        src = words[:, 256 * l + u : 256 * (l + 1) : 2]
+                    nc.tensor.transpose(bank[:, NP * s : NP * (s + 1)], src, ident[:])
+
+        def a2_out(g, t):
+            nc.scalar.copy(
+                out=a2_turned[:, g % 2, 1024 * t : 1024 * (t + 1)]
+                .bitcast(F32)
+                .rearrange("p (l r u) -> p l r u", l=LG, u=2),
+                in_=bank_of[("a2", g, t)][:].rearrange("p (l u r) -> p l r u", l=LG, u=2),
+            )
+
+        def a2_quant(g, ts):
+            words = slice(256 * ts[0], 256 * (ts[-1] + 1))
+            values = slice(1024 * ts[0], 1024 * (ts[-1] + 1))
+            quantize(a2_codes[:, g % 2, words], a2_scales[:, g % 2, words], a2_turned[:, g % 2, values])
+
+        def j2_pass(out, g, t, l, cols):
+            rows = slice(NP * (LG * t + l), NP * (LG * t + l + 1))
+            nc.tensor.matmul_mx(
+                out=out,
+                lhsT=a2_codes[:, g % 2, rows].bitcast(FP8X4),
+                lhsT_scale=a2_scales[:, g % 2, rows],
+                rhs=b2_codes[:, l, 2 * cols.start : 2 * cols.stop].bitcast(FP4X4),
+                rhs_scale=b2_plane[:, l, cols],
+                start=(l == 0),
+                stop=(l == LG - 1),
+            )
+
+        def j2(g, chunks):
+            for c in chunks:
+                next_bank(("j2", g, c))
+            for t in range(4):
+                for l in range(LG):
+                    for c in chunks:
+                        out = bank_of[("j2", g, c)][:, NP * t : NP * (t + 1)]
+                        j2_pass(out, g, t, l, slice(NP * c, NP * (c + 1)))
+
+        def j2t(g, chunks, t):
+            for l in range(LG):
+                for c in chunks:
+                    bank = next_bank(("j2", g, c)) if t == 0 and l == 0 else bank_of[("j2", g, c)]
+                    j2_pass(bank[:, NP * t : NP * (t + 1)], g, t, l, slice(NP * c, NP * (c + 1)))
+
+        def j2_out(g, c):
+            nc.vector.tensor_tensor(
+                out=v2_woven[:, g % 2, 512 * c : 512 * (c + 1)].rearrange("p (n t) -> p n t", t=4),
+                in0=bank_of[("j2", g, c)][:].rearrange("p (t n) -> p n t", t=4),
+                in1=weight[:, g, :].unsqueeze(1).to_broadcast([NP, NP, 4]),
+                op=ALU.mult,
+            )
+
+        def j2w(g, h, t):
+            bank = next_bank(("j2w", g, h, t))
+            for l in range(LG):
+                j2_pass(bank[:], g, t, l, slice(512 * h, 512 * (h + 1)))
+
+        def j2w_out(g, h, t):
+            nc.scalar.activation(
+                out=v2_slots[:, t, :], in_=bank_of[("j2w", g, h, t)][:], func=ACT.Copy, scale=weight[:, g, t : t + 1]
+            )
+
+        def v2_weave(g, h, engine, part, parts):
+            n = 512 // parts
+            start = 2048 * h + 4 * n * part
+            weave(engine, v2_woven[:, g % 2, start : start + 4 * n], v2_slots[:, :, n * part : n * (part + 1)])
+
+        def v2_quant(g, chunks):
+            words = slice(NP * chunks[0], NP * (chunks[-1] + 1))
+            values = slice(512 * chunks[0], 512 * (chunks[-1] + 1))
+            quantize(v2_codes[:, g, words], v2_scales[:, g, words], v2_woven[:, g % 2, values])
+
+        def b1_weave(k, engine):
+            weave(engine, b1_woven[:, k, :], b1_raw[:, k])
+
+        def b1_quant(k):
+            quantize(b1_codes[:, k, :], b1_scales[:, k, :], b1_woven[:, k, :])
+
+        def f1_scales_step():
+            nc.vector.tensor_copy(
+                out=f1_plane[:].rearrange("p t g c -> p t (g c)").bitcast(I32).rearrange("p t (j i) -> p t j i", i=2),
+                in_=f1_plane_raw[:].bitcast(I32).rearrange("p (j t i) -> p t j i", t=4, i=2),
+            )
+
+        def f1_words_step(g):
+            nc.vector.tensor_copy(
+                out=f1_codes[:, g % 2].rearrange("p t k (j i) -> p t (k j) i", i=8),
+                in_=f1_raw[g][:].rearrange("p (j t i) -> p t j i", t=4, i=8),
+            )
+
+        def j1_passes(out, g, t, cols):
+            for k in range(KG):
+                nc.tensor.matmul_mx(
+                    out=out,
+                    lhsT=f1_codes[:, g % 2, t, k, :].bitcast(FP8X4),
+                    lhsT_scale=f1_plane[4 * k : NP, t, g, :],
+                    rhs=b1_codes[:, k, cols].bitcast(FP8X4),
+                    rhs_scale=b1_scales[:, k, cols],
+                    start=(k == 0),
+                    stop=(k == KG - 1),
+                )
+
+        def j1(g, t):
+            j1_passes(next_bank(("j1", g, t))[:], g, t, slice(0, P))
+
+        def j1h(g, half, pair):
+            bank = next_bank(("j1h", g, half, pair))
+            for n in range(2):
+                j1_passes(bank[:, 256 * n : 256 * (n + 1)], g, 2 * pair + n, slice(256 * half, 256 * (half + 1)))
+
+        def j1h_out(g, half, pair):
+            for n in range(2):
+                t = 2 * pair + n
+                nc.scalar.activation(
+                    out=v1_slots[:, g % 2, t, 256 * half : 256 * (half + 1)],
+                    in_=bank_of[("j1h", g, half, pair)][:, 256 * n : 256 * (n + 1)],
+                    func=ACT.Copy,
+                    scale=vec_cols[:, t, g : g + 1],
+                )
+
+        def j1_out(g, t):
+            nc.scalar.activation(
+                out=v1_slots[:, g % 2, t, :],
+                in_=bank_of[("j1", g, t)][:],
+                func=ACT.Copy,
+                scale=vec_cols[:, t, g : g + 1],
+            )
+
+        def v1_weave(g, half, engine):
+            weave(
+                engine,
+                v1_woven[:, g % 2, 1024 * half : 1024 * (half + 1)],
+                v1_slots[:, g % 2, :, 256 * half : 256 * (half + 1)],
+            )
+
+        def v1_quant(g, halves):
+            words = slice(256 * halves[0], 256 * (halves[-1] + 1))
+            values = slice(1024 * halves[0], 1024 * (halves[-1] + 1))
+            quantize(v1_codes[:, g, words], v1_scales[:, g, words], v1_woven[:, g % 2, values])
+
+        def h_passes(h, j, groups):
+            bank = next_bank(("h", h, j)) if groups[0] == 0 else bank_of[("h", h, j)]
+            rows = slice(NP * j, NP * (j + 1))
+            cols = slice(512 * h, 512 * (h + 1))
+            for g in groups:
+                nc.tensor.matmul_mx(
+                    out=bank[:],
+                    lhsT=v1_codes[:, g, rows].bitcast(FP8X4),
+                    lhsT_scale=v1_scales[:, g, rows],
+                    rhs=v2_codes[:, g, cols].bitcast(FP8X4),
+                    rhs_scale=v2_scales[:, g, cols],
+                    start=(g == 0),
+                    stop=(g == EG - 1),
+                )
+
+        def hh_passes(h, j, part):
+            bank = next_bank(("hh", h, j, part))
+            rows = slice(NP * j, NP * (j + 1))
+            cols = slice(512 * h + 256 * part, 512 * h + 256 * (part + 1))
+            for g in range(EG):
+                nc.tensor.matmul_mx(
+                    out=bank[:, 0:256],
+                    lhsT=v1_codes[:, g, rows].bitcast(FP8X4),
+                    lhsT_scale=v1_scales[:, g, rows],
+                    rhs=v2_codes[:, g, cols].bitcast(FP8X4),
+                    rhs_scale=v2_scales[:, g, cols],
+                    start=(g == 0),
+                    stop=(g == EG - 1),
+                )
+
+        def hh_add(h, j, part):
+            c = part_of(part)
+            nc.vector.tensor_tensor(
+                out=h_sum[:, j % 2, c],
+                in0=bank_of[("hh", h, j, part)][:, 0:256],
+                in1=h0[:, j, 512 * h + c.start : 512 * h + c.stop],
+                op=ALU.add,
+            )
+
+        def part_of(part):
+            return slice(0, 512) if part is None else slice(256 * part, 256 * (part + 1))
+
+        def h_add(h, j, part=None):
+            c = part_of(part)
+            nc.vector.tensor_tensor(
+                out=h_sum[:, j % 2, c],
+                in0=bank_of[("h", h, j)][:, c],
+                in1=h0[:, j, 512 * h + c.start : 512 * h + c.stop],
+                op=ALU.add,
+            )
+
+        def y_scale(h, j, part=None):
+            c = part_of(part)
+            nc.vector.scalar_tensor_tensor(
+                out=y_of(h)[:, j, c],
+                in0=h_sum[:, j % 2, c],
+                scalar=vec_cols[:, j, UNIT1_ROW : UNIT1_ROW + 1],
+                in1=unit2_rows[:, 512 * h + c.start : 512 * h + c.stop],
+                op0=ALU.mult,
+                op1=ALU.mult,
+            )
+
+        def y_direct(h, j, u):
+            def pairs(ap):
+                return ap.rearrange("p (m u e) -> p u m e", u=2, e=2)[:, u]
+
+            nc.vector.scalar_tensor_tensor(
+                out=y_round()[:, h, j, 256 * u : 256 * (u + 1)].rearrange("p (m e) -> p m e", e=2),
+                in0=pairs(h_sum[:, j % 2, :]),
+                scalar=vec_cols[:, j, UNIT1_ROW : UNIT1_ROW + 1],
+                in1=pairs(unit2_rows[:, 512 * h : 512 * (h + 1)]),
+                op0=ALU.mult,
+                op1=ALU.mult,
+            )
+
+        def units(j):
+            nc.scalar.activation(
+                out=reuse("units%d" % j, [NP, Q], F32, "f1_raw%d" % j)[:],
+                in_=unit2_rows[:],
+                func=ACT.Copy,
+                scale=vec_cols[:, j, UNIT1_ROW : UNIT1_ROW + 1],
+            )
+
+        def y_scale_g(h, j):
+            nc.gpsimd.tensor_tensor(
+                out=y_of(h)[:, j, :],
+                in0=h_sum[:, j % 2, :],
+                in1=late["units%d" % j][:, 512 * h : 512 * (h + 1)],
+                op=ALU.mult,
+            )
+
+        def y_store(h, j):
+            nc.sync.dma_start(out=out_0[NP * j : NP * (j + 1), 512 * h : 512 * (h + 1)], in_=y_of(h)[:, j, :])
+
+        def y_round_step(h, j, part=None):
+            c = part_of(part)
+            m = slice(c.start // 4, c.stop // 4)
+            nc.scalar.copy(
+                out=y_round()[:, h, j, :].rearrange("p (u m e) -> p u m e", u=2, e=2)[:, :, m, :],
+                in_=y_of(h)[:, j, c].rearrange("p (m u e) -> p u m e", u=2, e=2),
+            )
+
+        def y_turn(h, tiles):
+            bank = next_bank(("y", h, tiles))
+            for n, j in enumerate(tiles):
+                words = y_round()[:, h, j, :].bitcast(F32)
+                for u in range(2):
+                    s = 2 * n + u
+                    nc.tensor.transpose(bank[:, NP * s : NP * (s + 1)], words[:, NP * u : NP * (u + 1)], ident[:])
+
+        def y_out(h, tiles, engine="S"):
+            n = len(tiles)
+            copy_on(
+                engine,
+                y_turned()[:, h, 512 * tiles[0] : 512 * (tiles[-1] + 1)]
+                .bitcast(F32)
+                .rearrange("p (n r u) -> p n r u", n=n, u=2),
+                bank_of[("y", h, tiles)][:, 0 : 256 * n].rearrange("p (n u r) -> p n r u", n=n, u=2),
+            )
+
+        def y_quant(h, tiles):
+            words = slice(NP * tiles[0], NP * (tiles[-1] + 1))
+            values = slice(512 * tiles[0], 512 * (tiles[-1] + 1))
+            quantize(y_codes[:, h, words], y_scales[:, h, words], y_turned()[:, h, values])
+
+        def words_store(h, tiles):
+            words = slice(NP * tiles[0], NP * (tiles[-1] + 1))
+            nc.sync.dma_start(
+                out=out_1[h].rearrange("p m t -> p (m t)").bitcast(I32)[:, words],
+                in_=y_codes[:, h, words].bitcast(I32),
+            )
+
+        def scales_store(halves, quad):
+            hs = slice(halves[0], halves[-1] + 1)
+            queue = nc.sync if quad % 2 == 0 else nc.scalar
+            queue.dma_start(
+                out=out_2.bitcast(I32).rearrange("h r m -> r h m")[4 * quad : 4 * quad + 4, hs],
+                in_=y_scales[32 * quad : 32 * quad + 4, hs].bitcast(I32),
+            )
+
+        steps = {
+            "load": load, "clear": clear, "vec_stage": vec_stage, "vec_turn": vec_turn, "vec_out": vec_out,
+            "a2_split": a2_split, "a2_turn": a2_turn, "a2_out": a2_out, "a2_quant": a2_quant,
+            "j2": j2, "j2_out": j2_out, "v2_quant": v2_quant, "j2w": j2w, "j2w_out": j2w_out, "v2_weave": v2_weave,
+            "b1_weave": b1_weave, "b1_quant": b1_quant, "f1_scales": f1_scales_step, "f1_words": f1_words_step,
+            "j1": j1, "j1_out": j1_out, "v1_weave": v1_weave, "v1_quant": v1_quant,
+            "h": h_passes, "h_add": h_add, "y_scale": y_scale, "y_store": y_store, "y_round": y_round_step,
+            "y_turn": y_turn, "y_out": y_out, "y_quant": y_quant,
+            "ident": ident_step, "warm_prep": warm_prep, "warm": warm, "y_direct": y_direct, "hh": hh_passes, "hh_add": hh_add, "warm_quant": warm_quant, "j2t": j2t, "j1h": j1h, "j1h_out": j1h_out,
+            "units": units, "y_scale_g": y_scale_g, "words_store": words_store, "scales_store": scales_store,
+        }
+        for step in program_order():
+            steps[step[0]](*step[1:])

@@ -31,17 +31,17 @@ def program_order():
     def put(*steps):
         o.extend(steps)
 
-    put(("load", "vec", 0), ("load", "vec", 1), ("ident",))
+    put(("ident",), ("load", "vec", 0), ("load", "vec", 1), ("clear", "f1s", "G"))
     put(("warm_prep",), ("clear", "b2s", "V"), ("warm_quant",), ("warm", 10, 0))
-    put(("clear", "vec", "V"), ("clear", "f1s", "V"))
+    put(("clear", "vec", "V"))
     put(("load", "a2", 0, 0), ("load", "vec", 2), *[("load", "a2", 0, t) for t in (1, 2, 3)])
     put(("load", "b2w", 0), *[("load", "b2s", i) for i in range(4)], ("load", "b2w", 1))
-    put(*[("load", "a2", 1, t) for t in range(4)])
-    put(("load", "b1", 0), ("load", "b1", 1))
+    put(("load", "b1", 0), *[("load", "a2", 1, t) for t in range(4)])
+    put(("load", "b1", 1), ("load", "b1", 2))
     put(*[("load", "a2", 2, t) for t in range(4)])
-    put(("load", "b1", 2), *[("load", "f1s", i) for i in range(4)])
-    put(("load", "f1", 0), *[("load", "a2", 3, t) for t in range(4)])
-    put(("load", "f1", 1), ("load", "f1", 2), ("load", "f1", 3), ("load", "h0"), ("load", "u2"))
+    put(*[("load", "f1s", i) for i in range(4)])
+    put(("load", "f1", 0), ("load", "u2"), *[("load", "a2", 3, t) for t in range(4)])
+    put(("load", "f1", 1), ("load", "f1", 2), ("load", "f1", 3), ("load", "h0"))
 
     def split(g):
         if SPLIT and g >= SPLIT - 1:
@@ -66,37 +66,35 @@ def program_order():
 
     put(("vec_stage",))
     for t in range(4):
-        if t == 3:
-            put(("vec_turn",))
         put(("a2_turn", 0, t), ("a2_out", 0, t), ("a2_quant", 0, (t,)))
-    put(("vec_out",))
+    put(("vec_turn",), ("vec_out",))
     for t in range(4):
         put(("j2t", 0, (0, 1, 2, 3), t))
     split(1)
     put(*[("j2_out", 0, c) for c in range(4)])
-    put(("j2", 0, (4, 5)))
+    put(("j2", 0, (4, 5)), ("b1_weave", 0, "S"))
     turn(1)
     put(("j2_out", 0, 4), ("j2_out", 0, 5), ("a2_quant", 1, (0, 1)), ("a2_quant", 1, (2, 3)))
-    put(("b1_weave", 0, "S"))
+    put(("b1_weave", 1, "S"))
     split(2)
     j2_pair(0, 6)
-    put(("b1_weave", 1, "S"))
+    put(("b1_weave", 2, "S"))
     j2_pair(1, 0)
-    put(("b1_weave", 2, "V"), ("b1_quant", 0))
+    put(("b1_quant", 0))
     j2_pair(1, 2)
     turn(2)
-    put(("b1_quant", 2), ("f1_scales",), ("f1_words", 0), ("b1_quant", 1))
+    put(("b1_quant", 1), ("f1_scales",), ("f1_words", 0), ("b1_quant", 2))
     split(3)
     j2_pair(1, 4)
-    put(("v2_quant", 0, (0, 1, 2, 3)))
-    put(("a2_quant", 2, (0, 1)), ("a2_quant", 2, (2, 3)))
+    put(("a2_quant", 2, (0, 1, 2, 3)))
     j2_pair(1, 6)
-    put(("v2_quant", 0, (4, 5, 6, 7)), ("f1_words", 1))
+    put(("v2_quant", 0, tuple(range(8))), ("f1_words", 1))
+    put(("units", 0, 0), ("units", 0, 1))
     j1_slots(0, range(4))
     turn(3)
-    put(("v1_weave", 0, 0, "S"), ("v1_weave", 0, 1, "S"), ("v2_quant", 1, (0, 1, 2, 3)), ("f1_words", 2))
+    put(("v1_weave", 0, 0, "S"), ("v1_weave", 0, 1, "S"), ("f1_words", 2))
     j2_pair(2, 0)
-    put(("v2_quant", 1, (4, 5, 6, 7)), ("a2_quant", 3, (0, 1)), ("a2_quant", 3, (2, 3)), ("v1_quant", 0, (0, 1)))
+    put(("v2_quant", 1, tuple(range(8))), ("a2_quant", 3, (0, 1, 2, 3)), ("v1_quant", 0, (0, 1)))
     j1_slots(1, range(4))
     put(("v1_weave", 1, 0, "S"), ("v1_weave", 1, 1, "S"), ("f1_words", 3))
 
@@ -108,18 +106,19 @@ def program_order():
     j2_pair(2, 2)
     j1_pair(2, 0, 0)
     j2_pair(2, 4)
-    put(("v2_quant", 2, (0, 1, 2, 3)))
     j1_pair(2, 0, 1)
     j2_pair(2, 6)
     put(("v1_quant", 1, (0, 1)))
     j1_pair(3, 0, 0)
     j2_pair(3, 0)
-    put(("v2_quant", 2, (4, 5, 6, 7)))
+    put(("v2_quant", 2, tuple(range(8))))
     j1_pair(3, 0, 1)
+    put(("units", 1, 0), ("units", 1, 1))
     j2_pair(3, 2)
     put(("v1_quant", 2, (0,)))
     j2_pair(3, 4)
     put(("v2_quant", 3, (0, 1, 2, 3)), ("v1_quant", 3, (0,)))
+    put(("units", 0, 2), ("units", 0, 3))
     j1_pair(2, 1, 0)
     j2_pair(3, 6)
     j1_pair(2, 1, 1)
@@ -127,7 +126,7 @@ def program_order():
     def passes(h, j):
         put(("h", h, j, (0, 1, 2, 3)), ("h_add", h, j))
 
-    def finish(h, j, eng="y_scale"):
+    def finish(h, j, eng="y_scale_g"):
         put((eng, h, j), ("y_round", h, j), ("y_store", h, j))
 
     def planes(h, tiles):
@@ -144,24 +143,39 @@ def program_order():
         epilogue(h, j)
         put(("y_round", h, j), ("y_store", h, j))
 
-    passes(0, 0)
+    def epilogue(h, j):
+        put(("h_add", h, j, 0), ("h_add", h, j, 1), ("y_scale", h, j, 0), ("y_scale", h, j, 1))
+
+    def tile(h, j):
+        put(("h", h, j, (0, 1, 2, 3)), ("h_add", h, j), ("y_scale_g", h, j))
+
+    def send(h, j):
+        put(("y_round", h, j), ("y_store", h, j))
+
+    tile(0, 0)
     put(("v2_quant", 3, (4, 5, 6, 7)))
     j1_pair(3, 1, 0)
     j1_pair(3, 1, 1)
-    put(("y_scale", 0, 0), ("v1_quant", 2, (1,)), ("y_round", 0, 0), ("y_store", 0, 0))
-    whole(0, 1)
-    put(("h", 1, 0, (0, 1, 2, 3)), ("h_add", 1, 0), ("v1_quant", 3, (1,)))
-    finish(1, 0)
-    whole(1, 1)
-    whole(0, 2)
-    put(("h", 0, 3, (0, 1, 2, 3)))
-    epilogue(0, 3)
+    put(("v1_quant", 2, (1,)))
+    send(0, 0)
+    tile(0, 1)
+    put(("h", 1, 0, (0, 1, 2, 3)), ("h_add", 1, 0), ("v1_quant", 3, (1,)), ("y_scale_g", 1, 0))
+    send(0, 1)
+    tile(1, 1)
+    send(1, 0)
+    tile(0, 2)
+    send(1, 1)
+    tile(0, 3)
+    send(0, 2)
     put(("h", 1, 2, (0, 1, 2, 3)))
     planes(0, (0, 1))
-    put(("y_turn", 1, (0, 1)), ("y_round", 0, 3), ("y_store", 0, 3), ("y_out", 1, (0, 1)))
+    send(0, 3)
     epilogue(1, 2)
-    put(("hh", 1, 3, 0), ("hh", 1, 3, 1), ("y_turn", 0, (2, 3)))
-    put(("y_round", 1, 2), ("y_store", 1, 2), ("y_out", 0, (2, 3)), ("y_turn", 1, (2,)), ("y_out", 1, (2,)))
+    put(("hh", 1, 3, 0), ("hh", 1, 3, 1))
+    send(1, 2)
+    planes(1, (0, 1))
+    planes(0, (2, 3))
+    planes(1, (2,))
     put(("hh_add", 1, 3, 0), ("hh_add", 1, 3, 1), ("y_quant", 0, (0, 1)), ("words_store", 0, (0, 1)), ("y_direct", 1, 3, 0), ("y_direct", 1, 3, 1))
     planes(1, (3,))
     put(("y_scale", 1, 3), ("y_store", 1, 3))
@@ -234,7 +248,10 @@ def tile_robust_information_block_k4_kernel(
 
         h0 = sbuf("h0", [NP, PT, Q], BF16)
         unit2_rows = sbuf("unit2_rows", [NP, Q], BF16)
-        h_sum = sbuf("h_sum", [NP, 2, 512], F32)
+
+        def h_sum_of(h, j):
+            return reuse("h_sum", [NP, 4, 512], F32, "b1_raw")[:, (2 * h + j) % 4]
+
 
         def y_of(h):
             return reuse("y%d" % h, [NP, PT, 512], F32, "a2_raw%d" % h)
@@ -547,7 +564,7 @@ def tile_robust_information_block_k4_kernel(
         def hh_add(h, j, part):
             c = part_of(part)
             nc.vector.tensor_tensor(
-                out=h_sum[:, j % 2, c],
+                out=h_sum_of(h, j)[:, c],
                 in0=bank_of[("hh", h, j, part)][:, 0:256],
                 in1=h0[:, j, 512 * h + c.start : 512 * h + c.stop],
                 op=ALU.add,
@@ -559,7 +576,7 @@ def tile_robust_information_block_k4_kernel(
         def h_add(h, j, part=None):
             c = part_of(part)
             nc.vector.tensor_tensor(
-                out=h_sum[:, j % 2, c],
+                out=h_sum_of(h, j)[:, c],
                 in0=bank_of[("h", h, j)][:, c],
                 in1=h0[:, j, 512 * h + c.start : 512 * h + c.stop],
                 op=ALU.add,
@@ -569,7 +586,7 @@ def tile_robust_information_block_k4_kernel(
             c = part_of(part)
             nc.vector.scalar_tensor_tensor(
                 out=y_of(h)[:, j, c],
-                in0=h_sum[:, j % 2, c],
+                in0=h_sum_of(h, j)[:, c],
                 scalar=vec_cols[:, j, UNIT1_ROW : UNIT1_ROW + 1],
                 in1=unit2_rows[:, 512 * h + c.start : 512 * h + c.stop],
                 op0=ALU.mult,
@@ -582,28 +599,23 @@ def tile_robust_information_block_k4_kernel(
 
             nc.vector.scalar_tensor_tensor(
                 out=y_round()[:, h, j, 256 * u : 256 * (u + 1)].rearrange("p (m e) -> p m e", e=2),
-                in0=pairs(h_sum[:, j % 2, :]),
+                in0=pairs(h_sum_of(h, j)),
                 scalar=vec_cols[:, j, UNIT1_ROW : UNIT1_ROW + 1],
                 in1=pairs(unit2_rows[:, 512 * h : 512 * (h + 1)]),
                 op0=ALU.mult,
                 op1=ALU.mult,
             )
 
-        def units(j):
+        def units(h, j):
             nc.scalar.activation(
-                out=reuse("units%d" % j, [NP, Q], F32, "f1_raw%d" % j)[:],
-                in_=unit2_rows[:],
+                out=reuse("units", [NP, QG, PT, 512], F32, None)[:, h, j],
+                in_=unit2_rows[:, 512 * h : 512 * (h + 1)],
                 func=ACT.Copy,
                 scale=vec_cols[:, j, UNIT1_ROW : UNIT1_ROW + 1],
             )
 
         def y_scale_g(h, j):
-            nc.gpsimd.tensor_tensor(
-                out=y_of(h)[:, j, :],
-                in0=h_sum[:, j % 2, :],
-                in1=late["units%d" % j][:, 512 * h : 512 * (h + 1)],
-                op=ALU.mult,
-            )
+            nc.gpsimd.tensor_tensor(out=y_of(h)[:, j, :], in0=h_sum_of(h, j), in1=late["units"][:, h, j], op=ALU.mult)
 
         def y_store(h, j):
             nc.sync.dma_start(out=out_0[NP * j : NP * (j + 1), 512 * h : 512 * (h + 1)], in_=y_of(h)[:, j, :])

@@ -40,8 +40,8 @@ def program_order():
     put(("load", "b1", 1), ("load", "b1", 2))
     put(*[("load", "a2", 2, t) for t in range(4)])
     put(*[("load", "f1s", i) for i in range(4)])
-    put(("load", "f1", 0), ("load", "u2"), *[("load", "a2", 3, t) for t in range(4)])
-    put(("load", "f1", 1), ("load", "f1", 2), ("load", "f1", 3), ("load", "h0"))
+    put(("load", "f1", 0), *[("load", "a2", 3, t) for t in range(4)])
+    put(("load", "f1", 1), ("load", "f1", 2), ("load", "f1", 3), ("load", "h0"), ("load", "u2"))
 
     def split(g):
         if SPLIT and g >= SPLIT - 1:
@@ -65,9 +65,9 @@ def program_order():
         put(("v1_weave", g, half, "S"))
 
     put(("vec_stage",))
-    for t in range(4):
-        put(("a2_turn", 0, t), ("a2_out", 0, t), ("a2_quant", 0, (t,)))
-    put(("vec_turn",), ("vec_out",))
+    turn(0)
+    put(("vec_turn",), ("a2_quant", 0, (0,)), ("a2_quant", 0, (1,)), ("a2_quant", 0, (2,)), ("vec_step", 0))
+    put(("a2_quant", 0, (3,)), ("vec_step", 1), ("vec_step", 2), ("vec_step", 3))
     for t in range(4):
         put(("j2t", 0, (0, 1, 2, 3), t))
     split(1)
@@ -89,7 +89,6 @@ def program_order():
     put(("a2_quant", 2, (0, 1, 2, 3)))
     j2_pair(1, 6)
     put(("v2_quant", 0, tuple(range(8))), ("f1_words", 1))
-    put(("units", 0, 0), ("units", 0, 1))
     j1_slots(0, range(4))
     turn(3)
     put(("v1_weave", 0, 0, "S"), ("v1_weave", 0, 1, "S"), ("f1_words", 2))
@@ -113,12 +112,10 @@ def program_order():
     j2_pair(3, 0)
     put(("v2_quant", 2, tuple(range(8))))
     j1_pair(3, 0, 1)
-    put(("units", 1, 0), ("units", 1, 1))
     j2_pair(3, 2)
     put(("v1_quant", 2, (0,)))
     j2_pair(3, 4)
     put(("v2_quant", 3, (0, 1, 2, 3)), ("v1_quant", 3, (0,)))
-    put(("units", 0, 2), ("units", 0, 3))
     j1_pair(2, 1, 0)
     j2_pair(3, 6)
     j1_pair(2, 1, 1)
@@ -126,7 +123,7 @@ def program_order():
     def passes(h, j):
         put(("h", h, j, (0, 1, 2, 3)), ("h_add", h, j))
 
-    def finish(h, j, eng="y_scale_g"):
+    def finish(h, j, eng="y_scale"):
         put((eng, h, j), ("y_round", h, j), ("y_store", h, j))
 
     def planes(h, tiles):
@@ -152,36 +149,42 @@ def program_order():
     def send(h, j):
         put(("y_round", h, j), ("y_store", h, j))
 
-    tile(0, 0)
+    def add(h, j):
+        put(("h", h, j, (0, 1, 2, 3)), ("h_add", h, j))
+
+    def scale(h, j):
+        put(("y_scale", h, j))
+        send(h, j)
+
+    add(0, 0)
     put(("v2_quant", 3, (4, 5, 6, 7)))
     j1_pair(3, 1, 0)
     j1_pair(3, 1, 1)
+    scale(0, 0)
+    add(0, 1)
     put(("v1_quant", 2, (1,)))
-    send(0, 0)
-    tile(0, 1)
-    put(("h", 1, 0, (0, 1, 2, 3)), ("h_add", 1, 0), ("v1_quant", 3, (1,)), ("y_scale_g", 1, 0))
-    send(0, 1)
-    tile(1, 1)
-    send(1, 0)
-    tile(0, 2)
-    send(1, 1)
-    tile(0, 3)
-    send(0, 2)
-    put(("h", 1, 2, (0, 1, 2, 3)))
-    planes(0, (0, 1))
-    send(0, 3)
-    epilogue(1, 2)
-    put(("hh", 1, 3, 0), ("hh", 1, 3, 1))
-    send(1, 2)
-    planes(1, (0, 1))
-    planes(0, (2, 3))
-    planes(1, (2,))
-    put(("hh_add", 1, 3, 0), ("hh_add", 1, 3, 1), ("y_quant", 0, (0, 1)), ("words_store", 0, (0, 1)), ("y_direct", 1, 3, 0), ("y_direct", 1, 3, 1))
-    planes(1, (3,))
+    scale(0, 1)
+    add(1, 0)
+    put(("v1_quant", 3, (1,)))
+    scale(1, 0)
+    add(1, 1)
+    add(0, 2)
+    scale(1, 1)
+    add(0, 3)
+    scale(0, 2)
+    add(1, 2)
+    put(("y_turn", 0, (0, 1)), ("hh", 1, 3, 0), ("hh", 1, 3, 1), ("y_turn", 1, (0, 1)), ("y_out", 0, (0, 1)))
+    scale(0, 3)
+    put(("y_out", 1, (0, 1)), ("y_turn", 0, (2, 3)))
+    put(("hh_add", 1, 3, 0), ("hh_add", 1, 3, 1))
+    scale(1, 2)
+    put(("y_direct", 1, 3, 0), ("y_direct", 1, 3, 1), ("y_out", 0, (2, 3)))
+    planes_out(0, (0, 1))
+    planes(1, (2, 3))
     put(("y_scale", 1, 3), ("y_store", 1, 3))
     planes_out(1, (0, 1))
-    put(("y_quant", 0, (2, 3)), ("words_store", 0, (2, 3)))
-    put(("y_quant", 1, (2, 3)), ("words_store", 1, (2, 3)))
+    planes_out(0, (2, 3))
+    planes_out(1, (2, 3))
     put(*[("scales_store", (0, 1), i) for i in range(4)])
     return o
 
@@ -221,7 +224,7 @@ def tile_robust_information_block_k4_kernel(
         weight = sbuf("weight", [NP, EG, 4], F32)
 
         a2_raw = [sbuf("a2_raw%d" % g, [NP, 4, L], BF16) for g in range(EG)]
-        a2_even_odd = sbuf("a2_even_odd", [NP, 2, 4, L // 2], F32) if SPLIT else None
+        a2_even_odd = sbuf("a2_even_odd", [NP, 4, L // 2], F32) if SPLIT else None
         a2_turned = sbuf("a2_turned", [NP, 2, 4 * LG * NP * 4], BF16)
         a2_codes = sbuf("a2_codes", [NP, 2, 4 * LG * NP], U32)
         a2_scales = sbuf("a2_scales", [NP, 2, 4 * LG * NP], U8)
@@ -229,7 +232,7 @@ def tile_robust_information_block_k4_kernel(
         b2_plane = sbuf("b2_plane", [NP, LG, Q], U8)
 
         f1_raw = [sbuf("f1_raw%d" % g, [NP, KG * 512], I32) for g in range(EG)]
-        f1_codes = sbuf("f1_codes", [NP, 2, 4, KG, NP], I32)
+        f1_codes = sbuf("f1_codes", [NP, EG, 4, KG, NP], I32)
         f1_plane_raw = sbuf("f1_plane_raw", [NP, E], U8)
         f1_plane = sbuf("f1_plane", [NP, 4, EG, NP], U8)
         b1_raw = sbuf("b1_raw", [NP, KG, 4, P], BF16)
@@ -237,7 +240,10 @@ def tile_robust_information_block_k4_kernel(
         b1_codes = sbuf("b1_codes", [NP, KG, P], U32)
         b1_scales = sbuf("b1_scales", [NP, KG, P], U8)
 
-        v1_slots = sbuf("v1_slots", [NP, 2, 4, P], BF16)
+
+        def v1_slots():
+            return reuse("v1_slots", [NP, 2, 4, P], BF16, "b1_woven")
+
         v1_woven = sbuf("v1_woven", [NP, 2, P * 4], BF16)
         v1_codes = sbuf("v1_codes", [NP, EG, P], U32)
         v1_scales = sbuf("v1_scales", [NP, EG, P], U8)
@@ -366,20 +372,24 @@ def tile_robust_information_block_k4_kernel(
             for t in range(4):
                 nc.tensor.transpose(bank[:, NP * t : NP * (t + 1)], vec_rows[:, t, :], ident[:])
 
-        def vec_out():
-            bank = bank_of["vec"][:].rearrange("p (t c) -> p t c", t=4)
-            nc.vector.tensor_copy(out=vec_cols[:], in_=bank[:, :, 0 : UNIT1_ROW + 1])
-            r = vec_cols[:, :, EG : 2 * EG].rearrange("p t g -> p g t")
-            nc.vector.scalar_tensor_tensor(
-                out=cauchy_sq[:], in0=r, scalar=1.0 / (CAUCHY * CAUCHY), in1=r, op0=ALU.mult, op1=ALU.mult
-            )
-            nc.vector.tensor_scalar_add(out=cauchy_den[:], in0=cauchy_sq[:], scalar1=1.0)
-            nc.vector.reciprocal(out=weight[:], in_=cauchy_den[:])
+        def vec_step(n):
+            if n == 0:
+                bank = bank_of["vec"][:].rearrange("p (t c) -> p t c", t=4)
+                nc.vector.tensor_copy(out=vec_cols[:], in_=bank[:, :, 0 : UNIT1_ROW + 1])
+            elif n == 1:
+                r = vec_cols[:, :, EG : 2 * EG].rearrange("p t g -> p g t")
+                nc.vector.scalar_tensor_tensor(
+                    out=cauchy_sq[:], in0=r, scalar=1.0 / (CAUCHY * CAUCHY), in1=r, op0=ALU.mult, op1=ALU.mult
+                )
+            elif n == 2:
+                nc.vector.tensor_scalar_add(out=cauchy_den[:], in0=cauchy_sq[:], scalar1=1.0)
+            else:
+                nc.vector.reciprocal(out=weight[:], in_=cauchy_den[:])
 
         def a2_split(g, t, engine):
             copy_on(
                 engine,
-                a2_even_odd[:, g % 2, t, :].rearrange("p (l u m) -> p l u m", l=LG, u=2),
+                a2_even_odd[:, t, :].rearrange("p (l u m) -> p l u m", l=LG, u=2),
                 a2_raw[g][:, t, :].bitcast(F32).rearrange("p (l m u) -> p l u m", l=LG, u=2),
             )
 
@@ -389,8 +399,8 @@ def tile_robust_information_block_k4_kernel(
             for l in range(LG):
                 for u in range(2):
                     s = 2 * l + u
-                    if SPLIT and g >= SPLIT - 1:
-                        src = a2_even_odd[:, g % 2, t, NP * s : NP * (s + 1)]
+                    if any(z[:3] == ("a2_split", g, t) for z in program_order()):
+                        src = a2_even_odd[:, t, NP * s : NP * (s + 1)]
                     else:
                         src = words[:, 256 * l + u : 256 * (l + 1) : 2]
                     nc.tensor.transpose(bank[:, NP * s : NP * (s + 1)], src, ident[:])
@@ -437,9 +447,9 @@ def tile_robust_information_block_k4_kernel(
 
         def j2_out(g, c):
             nc.vector.tensor_tensor(
-                out=v2_woven[:, g % 2, 512 * c : 512 * (c + 1)].rearrange("p (n t) -> p n t", t=4),
-                in0=bank_of[("j2", g, c)][:].rearrange("p (t n) -> p n t", t=4),
-                in1=weight[:, g, :].unsqueeze(1).to_broadcast([NP, NP, 4]),
+                out=v2_woven[:, g % 2, 512 * c : 512 * (c + 1)].rearrange("p (n i t) -> p n t i", i=2, t=4),
+                in0=bank_of[("j2", g, c)][:].rearrange("p (t n i) -> p n t i", t=4, i=2),
+                in1=weight[:, g, :].unsqueeze(1).unsqueeze(3).to_broadcast([NP, NP // 2, 4, 2]),
                 op=ALU.mult,
             )
 
@@ -477,7 +487,7 @@ def tile_robust_information_block_k4_kernel(
 
         def f1_words_step(g):
             nc.vector.tensor_copy(
-                out=f1_codes[:, g % 2].rearrange("p t k (j i) -> p t (k j) i", i=8),
+                out=f1_codes[:, g].rearrange("p t k (j i) -> p t (k j) i", i=8),
                 in_=f1_raw[g][:].rearrange("p (j t i) -> p t j i", t=4, i=8),
             )
 
@@ -485,7 +495,7 @@ def tile_robust_information_block_k4_kernel(
             for k in range(KG):
                 nc.tensor.matmul_mx(
                     out=out,
-                    lhsT=f1_codes[:, g % 2, t, k, :].bitcast(FP8X4),
+                    lhsT=f1_codes[:, g, t, k, :].bitcast(FP8X4),
                     lhsT_scale=f1_plane[4 * k : NP, t, g, :],
                     rhs=b1_codes[:, k, cols].bitcast(FP8X4),
                     rhs_scale=b1_scales[:, k, cols],
@@ -505,7 +515,7 @@ def tile_robust_information_block_k4_kernel(
             for n in range(2):
                 t = 2 * pair + n
                 nc.scalar.activation(
-                    out=v1_slots[:, g % 2, t, 256 * half : 256 * (half + 1)],
+                    out=v1_slots()[:, g % 2, t, 256 * half : 256 * (half + 1)],
                     in_=bank_of[("j1h", g, half, pair)][:, 256 * n : 256 * (n + 1)],
                     func=ACT.Copy,
                     scale=vec_cols[:, t, g : g + 1],
@@ -513,7 +523,7 @@ def tile_robust_information_block_k4_kernel(
 
         def j1_out(g, t):
             nc.scalar.activation(
-                out=v1_slots[:, g % 2, t, :],
+                out=v1_slots()[:, g % 2, t, :],
                 in_=bank_of[("j1", g, t)][:],
                 func=ACT.Copy,
                 scale=vec_cols[:, t, g : g + 1],
@@ -523,7 +533,7 @@ def tile_robust_information_block_k4_kernel(
             weave(
                 engine,
                 v1_woven[:, g % 2, 1024 * half : 1024 * (half + 1)],
-                v1_slots[:, g % 2, :, 256 * half : 256 * (half + 1)],
+                v1_slots()[:, g % 2, :, 256 * half : 256 * (half + 1)],
             )
 
         def v1_quant(g, halves):
@@ -667,7 +677,7 @@ def tile_robust_information_block_k4_kernel(
             )
 
         steps = {
-            "load": load, "clear": clear, "vec_stage": vec_stage, "vec_turn": vec_turn, "vec_out": vec_out,
+            "load": load, "clear": clear, "vec_stage": vec_stage, "vec_turn": vec_turn, "vec_step": vec_step,
             "a2_split": a2_split, "a2_turn": a2_turn, "a2_out": a2_out, "a2_quant": a2_quant,
             "j2": j2, "j2_out": j2_out, "v2_quant": v2_quant, "j2w": j2w, "j2w_out": j2w_out, "v2_weave": v2_weave,
             "b1_weave": b1_weave, "b1_quant": b1_quant, "f1_scales": f1_scales_step, "f1_words": f1_words_step,

from contextlib import ExitStack

import concourse.mybir as mybir
from concourse.masks import make_identity

E, K, L, P, Q = 2048, 1536, 1024, 512, 1024
CAUCHY = 2.3849
FLOPS = 2 * E * (K * P + L * Q + P * Q)

F32 = mybir.dt.float32
BF16 = mybir.dt.bfloat16
I32 = mybir.dt.int32
U32 = mybir.dt.uint32
U8 = mybir.dt.uint8
FP8X4 = mybir.dt.float8_e4m3fn_x4
FP4X4 = mybir.dt.float4_e2m1fn_x4
ALU = mybir.AluOpType
ACT = mybir.ActivationFunctionType

NP = 128
EG, KG, LG, QG, PT = E // 512, K // 512, L // 512, Q // 512, P // NP
UNIT1_ROW = 32


SPLIT = 0


def program_order():
    o = []

    def put(*steps):
        o.extend(steps)

    put(("ident",), ("load", "vec", 0), ("load", "vec", 1), ("clear", "f1s", "G"))
    put(("warm_prep",), ("clear", "b2s", "V"), ("warm_quant",), ("warm", 10, 0))
    put(("clear", "vec", "V"))
    put(("load", "a2", 0, 0), ("load", "vec", 2), *[("load", "a2", 0, t) for t in (1, 2, 3)])
    put(("load", "b2w", 0), *[("load", "b2s", i) for i in range(4)], ("load", "b2w", 1))
    put(("load", "b1", 0), *[("load", "a2", 1, t) for t in range(4)])
    put(("load", "b1", 1), ("load", "b1", 2))
    put(*[("load", "a2", 2, t) for t in range(4)])
    put(*[("load", "f1s", i) for i in range(4)])
    put(("load", "f1", 0), *[("load", "a2", 3, t) for t in range(4)])
    put(("load", "f1", 1), ("load", "f1", 2), ("load", "f1", 3), ("load", "h0"), ("load", "u2"))

    def split(g):
        if SPLIT and g >= SPLIT - 1:
            for t in range(4):
                put(("a2_split", g, t, "SSSS"[t]))

    def turn(g):
        for t in range(4):
            put(("a2_turn", g, t), ("a2_out", g, t))

    def j2_pair(g, c):
        put(("j2", g, (c, c + 1)), ("j2_out", g, c), ("j2_out", g, c + 1))

    def j1_slots(g, ts):
        for t in ts:
            put(("j1", g, t), ("j1_out", g, t))

    def j1_half(g, half):
        for tp in range(2):
            put(("j1h", g, half, tp), ("j1h_out", g, half, tp))
        put(("v1_weave", g, half, "S"))

    put(("vec_stage",))
    turn(0)
    put(("vec_turn",), ("a2_quant", 0, (0,)), ("a2_quant", 0, (1,)), ("a2_quant", 0, (2,)), ("vec_step", 0))
    put(("a2_quant", 0, (3,)), ("vec_step", 1), ("vec_step", 2), ("vec_step", 3))
    for t in range(4):
        put(("j2t", 0, (0, 1, 2, 3), t))
    split(1)
    put(*[("j2_out", 0, c) for c in range(4)])
    put(("j2", 0, (4, 5)), ("b1_weave", 0, "S"))
    turn(1)
    put(("j2_out", 0, 4), ("j2_out", 0, 5), ("a2_quant", 1, (0, 1)), ("a2_quant", 1, (2, 3)))
    put(("b1_weave", 1, "S"))
    split(2)
    j2_pair(0, 6)
    put(("b1_weave", 2, "S"))
    j2_pair(1, 0)
    put(("b1_quant", 0))
    j2_pair(1, 2)
    turn(2)
    put(("b1_quant", 1), ("f1_scales",), ("f1_words", 0), ("b1_quant", 2))
    split(3)
    j2_pair(1, 4)
    put(("a2_quant", 2, (0, 1, 2, 3)))
    j2_pair(1, 6)
    put(("v2_quant", 0, tuple(range(8))), ("f1_words", 1))
    j1_slots(0, range(4))
    turn(3)
    put(("v1_weave", 0, 0, "S"), ("v1_weave", 0, 1, "S"), ("f1_words", 2))
    j2_pair(2, 0)
    put(("v2_quant", 1, tuple(range(8))), ("a2_quant", 3, (0, 1, 2, 3)), ("v1_quant", 0, (0, 1)))
    j1_slots(1, range(4))
    put(("v1_weave", 1, 0, "S"), ("v1_weave", 1, 1, "S"), ("f1_words", 3))

    def j1_pair(g, half, tp):
        put(("j1h", g, half, tp), ("j1h_out", g, half, tp))
        if tp == 1:
            put(("v1_weave", g, half, "S"))

    j2_pair(2, 2)
    j1_pair(2, 0, 0)
    j2_pair(2, 4)
    j1_pair(2, 0, 1)
    j2_pair(2, 6)
    put(("v1_quant", 1, (0, 1)))
    j1_pair(3, 0, 0)
    j2_pair(3, 0)
    put(("v2_quant", 2, tuple(range(8))))
    j1_pair(3, 0, 1)
    j2_pair(3, 2)
    put(("v1_quant", 2, (0,)))
    j2_pair(3, 4)
    put(("v2_quant", 3, (0, 1, 2, 3)), ("v1_quant", 3, (0,)))
    j1_pair(2, 1, 0)
    j2_pair(3, 6)
    j1_pair(2, 1, 1)

    def passes(h, j):
        put(("h", h, j, (0, 1, 2, 3)), ("h_add", h, j))

    def finish(h, j, eng="y_scale"):
        put((eng, h, j), ("y_round", h, j), ("y_store", h, j))

    def planes(h, tiles):
        put(("y_turn", h, tiles), ("y_out", h, tiles))

    def planes_out(h, tiles):
        put(("y_quant", h, tiles), ("words_store", h, tiles))

    def epilogue(h, j, add="h_add"):
        put((add, h, j, 0), (add, h, j, 1), ("y_scale", h, j, 0), ("y_scale", h, j, 1))

    def whole(h, j):
        put(("h", h, j, (0, 1, 2, 3)))
        epilogue(h, j)
        put(("y_round", h, j), ("y_store", h, j))

    def epilogue(h, j):
        put(("h_add", h, j, 0), ("h_add", h, j, 1), ("y_scale", h, j, 0), ("y_scale", h, j, 1))

    def tile(h, j):
        put(("h", h, j, (0, 1, 2, 3)), ("h_add", h, j), ("y_scale_g", h, j))

    def send(h, j):
        put(("y_round", h, j), ("y_store", h, j))

    def add(h, j):
        put(("h", h, j, (0, 1, 2, 3)), ("h_add", h, j))

    def scale(h, j):
        put(("y_scale", h, j))
        send(h, j)

    add(0, 0)
    put(("v2_quant", 3, (4, 5, 6, 7)))
    j1_pair(3, 1, 0)
    j1_pair(3, 1, 1)
    scale(0, 0)
    add(0, 1)
    put(("v1_quant", 2, (1,)))
    scale(0, 1)
    add(1, 0)
    put(("v1_quant", 3, (1,)))
    scale(1, 0)
    add(1, 1)
    add(0, 2)
    scale(1, 1)
    add(0, 3)
    scale(0, 2)
    add(1, 2)
    put(("y_turn", 0, (0, 1)), ("hh", 1, 3, 0), ("hh", 1, 3, 1), ("y_turn", 1, (0, 1)), ("y_out", 0, (0, 1)))
    scale(0, 3)
    put(("y_out", 1, (0, 1)), ("y_turn", 0, (2, 3)))
    put(("hh_add", 1, 3, 0), ("hh_add", 1, 3, 1))
    scale(1, 2)
    put(("y_direct", 1, 3, 0), ("y_direct", 1, 3, 1), ("y_out", 0, (2, 3)))
    planes_out(0, (0, 1))
    planes(1, (2, 3))
    put(("y_scale", 1, 3), ("y_store", 1, 3))
    planes_out(1, (0, 1))
    planes_out(0, (2, 3))
    planes_out(1, (2, 3))
    put(*[("scales_store", (0, 1), i) for i in range(4)])
    return o


def tile_robust_information_block_k4_kernel(
    tc, f1_words, f1_scales, B1, A2, b2_words, b2_scales, info, resid, H0, unit1, unit2, out_0, out_1, out_2
):
    nc = tc.nc
    with ExitStack() as ctx:
        keep = ctx.enter_context(tc.tile_pool(name="keep", bufs=1))
        psum = ctx.enter_context(tc.psum_pool(name="psum", bufs=1))
        ctx.enter_context(tc.manual_schedule())

        def sbuf(name, shape, dtype, tag=None):
            return keep.tile(shape, dtype, name=name, tag=tag or name, align_bytes=64)

        late = {}

        def reuse(name, shape, dtype, tag):
            if name not in late:
                late[name] = sbuf(name, shape, dtype, tag)
            return late[name]

        banks = [psum.tile([NP, 512], F32, name="bank%d" % b) for b in range(8)]
        bank_of = {}

        def next_bank(key):
            bank_of[key] = banks[len(bank_of) % len(banks)]
            return bank_of[key]

        ident = sbuf("ident", [NP, NP], F32)
        vec_raw = sbuf("vec_raw", [NP, 512], BF16)
        vec_rows = sbuf("vec_rows", [NP, 4, NP], F32)
        vec_cols = sbuf("vec_cols", [NP, 4, UNIT1_ROW + 1], F32)
        cauchy_sq = sbuf("cauchy_sq", [NP, EG, 4], F32)
        cauchy_den = sbuf("cauchy_den", [NP, EG, 4], F32)
        weight = sbuf("weight", [NP, EG, 4], F32)

        a2_raw = [sbuf("a2_raw%d" % g, [NP, 4, L], BF16) for g in range(EG)]
        a2_even_odd = sbuf("a2_even_odd", [NP, 4, L // 2], F32) if SPLIT else None
        a2_turned = sbuf("a2_turned", [NP, 2, 4 * LG * NP * 4], BF16)
        a2_codes = sbuf("a2_codes", [NP, 2, 4 * LG * NP], U32)
        a2_scales = sbuf("a2_scales", [NP, 2, 4 * LG * NP], U8)
        b2_codes = sbuf("b2_codes", [NP, LG, 2 * Q], U8)
        b2_plane = sbuf("b2_plane", [NP, LG, Q], U8)

        f1_raw = [sbuf("f1_raw%d" % g, [NP, KG * 512], I32) for g in range(EG)]
        f1_codes = sbuf("f1_codes", [NP, EG, 4, KG, NP], I32)
        f1_plane_raw = sbuf("f1_plane_raw", [NP, E], U8)
        f1_plane = sbuf("f1_plane", [NP, 4, EG, NP], U8)
        b1_raw = sbuf("b1_raw", [NP, KG, 4, P], BF16)
        b1_woven = sbuf("b1_woven", [NP, KG, P * 4], BF16)
        b1_codes = sbuf("b1_codes", [NP, KG, P], U32)
        b1_scales = sbuf("b1_scales", [NP, KG, P], U8)


        def v1_slots():
            return reuse("v1_slots", [NP, 2, 4, P], BF16, "b1_woven")

        v1_woven = sbuf("v1_woven", [NP, 2, P * 4], BF16)
        v1_codes = sbuf("v1_codes", [NP, EG, P], U32)
        v1_scales = sbuf("v1_scales", [NP, EG, P], U8)
        v2_slots = sbuf("v2_slots", [NP, 4, 512], BF16) if any(s[0] == "j2w" for s in program_order()) else None
        v2_woven = sbuf("v2_woven", [NP, 2, Q * 4], BF16)
        v2_codes = sbuf("v2_codes", [NP, EG, Q], U32)
        v2_scales = sbuf("v2_scales", [NP, EG, Q], U8)

        h0 = sbuf("h0", [NP, PT, Q], BF16)
        unit2_rows = sbuf("unit2_rows", [NP, Q], BF16)

        def h_sum_of(h, j):
            return reuse("h_sum", [NP, 4, 512], F32, "b1_raw")[:, (2 * h + j) % 4]


        def y_of(h):
            return reuse("y%d" % h, [NP, PT, 512], F32, "a2_raw%d" % h)

        def y_round():
            return reuse("y_round", [NP, QG, PT, 512], BF16, "a2_raw2")

        def y_turned():
            return reuse("y_turned", [NP, QG, P * 4], BF16, "a2_raw3")

        y_codes = sbuf("y_codes", [NP, QG, P], U32)
        y_scales = sbuf("y_scales", [NP, QG, P], U8)

        def copy_on(engine, out, in_):
            if engine == "S":
                nc.scalar.copy(out=out, in_=in_)
            else:
                nc.vector.tensor_copy(out=out, in_=in_)

        def weave(engine, woven, slots):
            copy_on(
                engine,
                woven.rearrange("p (c i t) -> p c t i", i=4, t=4),
                slots.rearrange("p t (c i) -> p c t i", i=4),
            )

        def quantize(codes, scales, values):
            nc.vector.quantize_mx(out=codes.bitcast(FP8X4), scales=scales, in_=values)

        def load(name, i=0, t=0):
            if name == "vec":
                src = [info, resid, unit1][i]
                rows = [slice(0, EG), slice(EG, 2 * EG), slice(UNIT1_ROW, UNIT1_ROW + 1)][i]
                queue = nc.gpsimd if i < 2 else nc.sync
                queue.dma_start(out=vec_raw[rows, :], in_=src.rearrange("(g e) -> g e", e=512))
            elif name == "a2":
                rows = A2[512 * i : 512 * (i + 1), :].rearrange("(j t i) k -> t j i k", t=4, i=8)
                nc.sync.dma_start(out=a2_raw[i][:, t, :], in_=rows[t])
            elif name == "b2w":
                cols = slice(256 * i, 256 * (i + 1))
                nc.sync.dma_start(
                    out=b2_codes[:].bitcast(I32)[:, :, cols],
                    in_=b2_words.bitcast(I32).rearrange("g p n -> p g n")[:, :, cols],
                )
            elif name == "b2s":
                nc.sync.dma_start(
                    out=b2_plane[32 * i : 32 * i + 4].bitcast(I32),
                    in_=b2_scales.bitcast(I32).rearrange("g r n -> r g n")[4 * i : 4 * i + 4],
                )
            elif name == "b1":
                nc.sync.dma_start(
                    out=b1_raw[:, i], in_=B1[512 * i : 512 * (i + 1), :].rearrange("(p t) c -> p t c", t=4)
                )
            elif name == "f1":
                words = f1_words.rearrange("g p n t -> p g (n t)").bitcast(I32)
                nc.sync.dma_start(
                    out=f1_raw[i][:].rearrange("p (g n) -> p g n", g=KG),
                    in_=words[:, :, 512 * i : 512 * (i + 1)],
                )
            elif name == "f1s":
                nc.sync.dma_start(
                    out=f1_plane_raw[32 * i : 32 * i + 4 * KG, :].bitcast(I32),
                    in_=f1_scales.bitcast(I32)[:, 4 * i : 4 * i + 4, :],
                )
            elif name == "h0":
                nc.sync.dma_start(out=h0[:], in_=H0.rearrange("(j p) q -> p j q", p=NP))
            else:
                nc.sync.dma_start(out=unit2_rows[:], in_=unit2.partition_broadcast(NP))

        def clear(name, engine):
            eng = nc.vector if engine == "V" else nc.gpsimd
            if name == "b2s":
                eng.memset(b2_plane[:].bitcast(I32), 0)
            elif name == "f1s":
                eng.memset(f1_plane_raw[:].bitcast(I32), 0)
            else:
                eng.memset(vec_rows[:], 0.0)

        def ident_step():
            make_identity(nc, ident[:])

        def warm_prep():
            nc.vector.memset(reuse("warm_zeros", [NP, 512], BF16, None)[:], 0.0)

        def warm_quant():
            quantize(
                reuse("warm_codes", [NP, NP], U32, None)[:],
                reuse("warm_scales", [NP, NP], U8, None)[:],
                late["warm_zeros"][:],
            )

        def warm(count, n):
            bank = next_bank(("warm", n))
            codes = late["warm_codes"][:].bitcast(FP8X4)
            scales = late["warm_scales"][:]
            for i in range(count):
                nc.tensor.matmul_mx(
                    out=bank[:, 0:NP], lhsT=codes, lhsT_scale=scales, rhs=codes, rhs_scale=scales,
                    start=(i == 0), stop=(i == count - 1),
                )

        def vec_stage():
            nc.vector.tensor_copy(
                out=vec_rows[0 : 2 * EG].rearrange("p t (j i) -> p t j i", i=8),
                in_=vec_raw[0 : 2 * EG, :].rearrange("p (j t i) -> p t j i", t=4, i=8),
            )
            row = slice(UNIT1_ROW, UNIT1_ROW + 1)
            nc.vector.tensor_copy(out=vec_rows[row].rearrange("p t c -> p (t c)"), in_=vec_raw[row, :])

        def vec_turn():
            bank = next_bank("vec")
            for t in range(4):
                nc.tensor.transpose(bank[:, NP * t : NP * (t + 1)], vec_rows[:, t, :], ident[:])

        def vec_step(n):
            if n == 0:
                bank = bank_of["vec"][:].rearrange("p (t c) -> p t c", t=4)
                nc.vector.tensor_copy(out=vec_cols[:], in_=bank[:, :, 0 : UNIT1_ROW + 1])
            elif n == 1:
                r = vec_cols[:, :, EG : 2 * EG].rearrange("p t g -> p g t")
                nc.vector.scalar_tensor_tensor(
                    out=cauchy_sq[:], in0=r, scalar=1.0 / (CAUCHY * CAUCHY), in1=r, op0=ALU.mult, op1=ALU.mult
                )
            elif n == 2:
                nc.vector.tensor_scalar_add(out=cauchy_den[:], in0=cauchy_sq[:], scalar1=1.0)
            else:
                nc.vector.reciprocal(out=weight[:], in_=cauchy_den[:])

        def a2_split(g, t, engine):
            copy_on(
                engine,
                a2_even_odd[:, t, :].rearrange("p (l u m) -> p l u m", l=LG, u=2),
                a2_raw[g][:, t, :].bitcast(F32).rearrange("p (l m u) -> p l u m", l=LG, u=2),
            )

        def a2_turn(g, t):
            bank = next_bank(("a2", g, t))
            words = a2_raw[g][:, t, :].bitcast(F32)
            for l in range(LG):
                for u in range(2):
                    s = 2 * l + u
                    if any(z[:3] == ("a2_split", g, t) for z in program_order()):
                        src = a2_even_odd[:, t, NP * s : NP * (s + 1)]
                    else:
                        src = words[:, 256 * l + u : 256 * (l + 1) : 2]
                    nc.tensor.transpose(bank[:, NP * s : NP * (s + 1)], src, ident[:])

        def a2_out(g, t):
            nc.scalar.copy(
                out=a2_turned[:, g % 2, 1024 * t : 1024 * (t + 1)]
                .bitcast(F32)
                .rearrange("p (l r u) -> p l r u", l=LG, u=2),
                in_=bank_of[("a2", g, t)][:].rearrange("p (l u r) -> p l r u", l=LG, u=2),
            )

        def a2_quant(g, ts):
            words = slice(256 * ts[0], 256 * (ts[-1] + 1))
            values = slice(1024 * ts[0], 1024 * (ts[-1] + 1))
            quantize(a2_codes[:, g % 2, words], a2_scales[:, g % 2, words], a2_turned[:, g % 2, values])

        def j2_pass(out, g, t, l, cols):
            rows = slice(NP * (LG * t + l), NP * (LG * t + l + 1))
            nc.tensor.matmul_mx(
                out=out,
                lhsT=a2_codes[:, g % 2, rows].bitcast(FP8X4),
                lhsT_scale=a2_scales[:, g % 2, rows],
                rhs=b2_codes[:, l, 2 * cols.start : 2 * cols.stop].bitcast(FP4X4),
                rhs_scale=b2_plane[:, l, cols],
                start=(l == 0),
                stop=(l == LG - 1),
            )

        def j2(g, chunks):
            for c in chunks:
                next_bank(("j2", g, c))
            for t in range(4):
                for l in range(LG):
                    for c in chunks:
                        out = bank_of[("j2", g, c)][:, NP * t : NP * (t + 1)]
                        j2_pass(out, g, t, l, slice(NP * c, NP * (c + 1)))

        def j2t(g, chunks, t):
            for l in range(LG):
                for c in chunks:
                    bank = next_bank(("j2", g, c)) if t == 0 and l == 0 else bank_of[("j2", g, c)]
                    j2_pass(bank[:, NP * t : NP * (t + 1)], g, t, l, slice(NP * c, NP * (c + 1)))

        def j2_out(g, c):
            nc.vector.tensor_tensor(
                out=v2_woven[:, g % 2, 512 * c : 512 * (c + 1)].rearrange("p (n i t) -> p n t i", i=2, t=4),
                in0=bank_of[("j2", g, c)][:].rearrange("p (t n i) -> p n t i", t=4, i=2),
                in1=weight[:, g, :].unsqueeze(1).unsqueeze(3).to_broadcast([NP, NP // 2, 4, 2]),
                op=ALU.mult,
            )

        def j2w(g, h, t):
            bank = next_bank(("j2w", g, h, t))
            for l in range(LG):
                j2_pass(bank[:], g, t, l, slice(512 * h, 512 * (h + 1)))

        def j2w_out(g, h, t):
            nc.scalar.activation(
                out=v2_slots[:, t, :], in_=bank_of[("j2w", g, h, t)][:], func=ACT.Copy, scale=weight[:, g, t : t + 1]
            )

        def v2_weave(g, h, engine, part, parts):
            n = 512 // parts
            start = 2048 * h + 4 * n * part
            weave(engine, v2_woven[:, g % 2, start : start + 4 * n], v2_slots[:, :, n * part : n * (part + 1)])

        def v2_quant(g, chunks):
            words = slice(NP * chunks[0], NP * (chunks[-1] + 1))
            values = slice(512 * chunks[0], 512 * (chunks[-1] + 1))
            quantize(v2_codes[:, g, words], v2_scales[:, g, words], v2_woven[:, g % 2, values])

        def b1_weave(k, engine):
            weave(engine, b1_woven[:, k, :], b1_raw[:, k])

        def b1_quant(k):
            quantize(b1_codes[:, k, :], b1_scales[:, k, :], b1_woven[:, k, :])

        def f1_scales_step():
            nc.vector.tensor_copy(
                out=f1_plane[:].rearrange("p t g c -> p t (g c)").bitcast(I32).rearrange("p t (j i) -> p t j i", i=2),
                in_=f1_plane_raw[:].bitcast(I32).rearrange("p (j t i) -> p t j i", t=4, i=2),
            )

        def f1_words_step(g):
            nc.vector.tensor_copy(
                out=f1_codes[:, g].rearrange("p t k (j i) -> p t (k j) i", i=8),
                in_=f1_raw[g][:].rearrange("p (j t i) -> p t j i", t=4, i=8),
            )

        def j1_passes(out, g, t, cols):
            for k in range(KG):
                nc.tensor.matmul_mx(
                    out=out,
                    lhsT=f1_codes[:, g, t, k, :].bitcast(FP8X4),
                    lhsT_scale=f1_plane[4 * k : NP, t, g, :],
                    rhs=b1_codes[:, k, cols].bitcast(FP8X4),
                    rhs_scale=b1_scales[:, k, cols],
                    start=(k == 0),
                    stop=(k == KG - 1),
                )

        def j1(g, t):
            j1_passes(next_bank(("j1", g, t))[:], g, t, slice(0, P))

        def j1h(g, half, pair):
            bank = next_bank(("j1h", g, half, pair))
            for n in range(2):
                j1_passes(bank[:, 256 * n : 256 * (n + 1)], g, 2 * pair + n, slice(256 * half, 256 * (half + 1)))

        def j1h_out(g, half, pair):
            for n in range(2):
                t = 2 * pair + n
                nc.scalar.activation(
                    out=v1_slots()[:, g % 2, t, 256 * half : 256 * (half + 1)],
                    in_=bank_of[("j1h", g, half, pair)][:, 256 * n : 256 * (n + 1)],
                    func=ACT.Copy,
                    scale=vec_cols[:, t, g : g + 1],
                )

        def j1_out(g, t):
            nc.scalar.activation(
                out=v1_slots()[:, g % 2, t, :],
                in_=bank_of[("j1", g, t)][:],
                func=ACT.Copy,
                scale=vec_cols[:, t, g : g + 1],
            )

        def v1_weave(g, half, engine):
            weave(
                engine,
                v1_woven[:, g % 2, 1024 * half : 1024 * (half + 1)],
                v1_slots()[:, g % 2, :, 256 * half : 256 * (half + 1)],
            )

        def v1_quant(g, halves):
            words = slice(256 * halves[0], 256 * (halves[-1] + 1))
            values = slice(1024 * halves[0], 1024 * (halves[-1] + 1))
            quantize(v1_codes[:, g, words], v1_scales[:, g, words], v1_woven[:, g % 2, values])

        def h_passes(h, j, groups):
            bank = next_bank(("h", h, j)) if groups[0] == 0 else bank_of[("h", h, j)]
            rows = slice(NP * j, NP * (j + 1))
            cols = slice(512 * h, 512 * (h + 1))
            for g in groups:
                nc.tensor.matmul_mx(
                    out=bank[:],
                    lhsT=v1_codes[:, g, rows].bitcast(FP8X4),
                    lhsT_scale=v1_scales[:, g, rows],
                    rhs=v2_codes[:, g, cols].bitcast(FP8X4),
                    rhs_scale=v2_scales[:, g, cols],
                    start=(g == 0),
                    stop=(g == EG - 1),
                )

        def hh_passes(h, j, part):
            bank = next_bank(("hh", h, j, part))
            rows = slice(NP * j, NP * (j + 1))
            cols = slice(512 * h + 256 * part, 512 * h + 256 * (part + 1))
            for g in range(EG):
                nc.tensor.matmul_mx(
                    out=bank[:, 0:256],
                    lhsT=v1_codes[:, g, rows].bitcast(FP8X4),
                    lhsT_scale=v1_scales[:, g, rows],
                    rhs=v2_codes[:, g, cols].bitcast(FP8X4),
                    rhs_scale=v2_scales[:, g, cols],
                    start=(g == 0),
                    stop=(g == EG - 1),
                )

        def hh_add(h, j, part):
            c = part_of(part)
            nc.vector.tensor_tensor(
                out=h_sum_of(h, j)[:, c],
                in0=bank_of[("hh", h, j, part)][:, 0:256],
                in1=h0[:, j, 512 * h + c.start : 512 * h + c.stop],
                op=ALU.add,
            )

        def part_of(part):
            return slice(0, 512) if part is None else slice(256 * part, 256 * (part + 1))

        def h_add(h, j, part=None):
            c = part_of(part)
            nc.vector.tensor_tensor(
                out=h_sum_of(h, j)[:, c],
                in0=bank_of[("h", h, j)][:, c],
                in1=h0[:, j, 512 * h + c.start : 512 * h + c.stop],
                op=ALU.add,
            )

        def y_scale(h, j, part=None):
            c = part_of(part)
            nc.vector.scalar_tensor_tensor(
                out=y_of(h)[:, j, c],
                in0=h_sum_of(h, j)[:, c],
                scalar=vec_cols[:, j, UNIT1_ROW : UNIT1_ROW + 1],
                in1=unit2_rows[:, 512 * h + c.start : 512 * h + c.stop],
                op0=ALU.mult,
                op1=ALU.mult,
            )

        def y_direct(h, j, u):
            def pairs(ap):
                return ap.rearrange("p (m u e) -> p u m e", u=2, e=2)[:, u]

            nc.vector.scalar_tensor_tensor(
                out=y_round()[:, h, j, 256 * u : 256 * (u + 1)].rearrange("p (m e) -> p m e", e=2),
                in0=pairs(h_sum_of(h, j)),
                scalar=vec_cols[:, j, UNIT1_ROW : UNIT1_ROW + 1],
                in1=pairs(unit2_rows[:, 512 * h : 512 * (h + 1)]),
                op0=ALU.mult,
                op1=ALU.mult,
            )

        def units(h, j):
            nc.scalar.activation(
                out=reuse("units", [NP, QG, PT, 512], F32, None)[:, h, j],
                in_=unit2_rows[:, 512 * h : 512 * (h + 1)],
                func=ACT.Copy,
                scale=vec_cols[:, j, UNIT1_ROW : UNIT1_ROW + 1],
            )

        def y_scale_g(h, j):
            nc.gpsimd.tensor_tensor(out=y_of(h)[:, j, :], in0=h_sum_of(h, j), in1=late["units"][:, h, j], op=ALU.mult)

        def y_store(h, j):
            nc.sync.dma_start(out=out_0[NP * j : NP * (j + 1), 512 * h : 512 * (h + 1)], in_=y_of(h)[:, j, :])

        def y_round_step(h, j, part=None):
            c = part_of(part)
            m = slice(c.start // 4, c.stop // 4)
            nc.scalar.copy(
                out=y_round()[:, h, j, :].rearrange("p (u m e) -> p u m e", u=2, e=2)[:, :, m, :],
                in_=y_of(h)[:, j, c].rearrange("p (m u e) -> p u m e", u=2, e=2),
            )

        def y_turn(h, tiles):
            bank = next_bank(("y", h, tiles))
            for n, j in enumerate(tiles):
                words = y_round()[:, h, j, :].bitcast(F32)
                for u in range(2):
                    s = 2 * n + u
                    nc.tensor.transpose(bank[:, NP * s : NP * (s + 1)], words[:, NP * u : NP * (u + 1)], ident[:])

        def y_out(h, tiles, engine="S"):
            n = len(tiles)
            copy_on(
                engine,
                y_turned()[:, h, 512 * tiles[0] : 512 * (tiles[-1] + 1)]
                .bitcast(F32)
                .rearrange("p (n r u) -> p n r u", n=n, u=2),
                bank_of[("y", h, tiles)][:, 0 : 256 * n].rearrange("p (n u r) -> p n r u", n=n, u=2),
            )

        def y_quant(h, tiles):
            words = slice(NP * tiles[0], NP * (tiles[-1] + 1))
            values = slice(512 * tiles[0], 512 * (tiles[-1] + 1))
            quantize(y_codes[:, h, words], y_scales[:, h, words], y_turned()[:, h, values])

        def words_store(h, tiles):
            words = slice(NP * tiles[0], NP * (tiles[-1] + 1))
            nc.sync.dma_start(
                out=out_1[h].rearrange("p m t -> p (m t)").bitcast(I32)[:, words],
                in_=y_codes[:, h, words].bitcast(I32),
            )

        def scales_store(halves, quad):
            hs = slice(halves[0], halves[-1] + 1)
            queue = nc.sync if quad % 2 == 0 else nc.scalar
            queue.dma_start(
                out=out_2.bitcast(I32).rearrange("h r m -> r h m")[4 * quad : 4 * quad + 4, hs],
                in_=y_scales[32 * quad : 32 * quad + 4, hs].bitcast(I32),
            )

        steps = {
            "load": load, "clear": clear, "vec_stage": vec_stage, "vec_turn": vec_turn, "vec_step": vec_step,
            "a2_split": a2_split, "a2_turn": a2_turn, "a2_out": a2_out, "a2_quant": a2_quant,
            "j2": j2, "j2_out": j2_out, "v2_quant": v2_quant, "j2w": j2w, "j2w_out": j2w_out, "v2_weave": v2_weave,
            "b1_weave": b1_weave, "b1_quant": b1_quant, "f1_scales": f1_scales_step, "f1_words": f1_words_step,
            "j1": j1, "j1_out": j1_out, "v1_weave": v1_weave, "v1_quant": v1_quant,
            "h": h_passes, "h_add": h_add, "y_scale": y_scale, "y_store": y_store, "y_round": y_round_step,
            "y_turn": y_turn, "y_out": y_out, "y_quant": y_quant,
            "ident": ident_step, "warm_prep": warm_prep, "warm": warm, "y_direct": y_direct, "hh": hh_passes, "hh_add": hh_add, "warm_quant": warm_quant, "j2t": j2t, "j1h": j1h, "j1h_out": j1h_out,
            "units": units, "y_scale_g": y_scale_g, "words_store": words_store, "scales_store": scales_store,
        }
        for step in program_order():
            steps[step[0]](*step[1:])
